import numpy as np
import ml_dtypes


def mxq(x, axis, fmt="e4m3"):
    dtype, down = {"e4m3": (ml_dtypes.float8_e4m3fn, 7), "e5m2": (ml_dtypes.float8_e5m2, 14)}[fmt]
    v = np.moveaxis(np.asarray(x, np.float32).astype(ml_dtypes.bfloat16).astype(np.float64), axis, -1)
    blocks = v.reshape(v.shape[:-1] + (-1, 32))
    amax = np.abs(blocks).max(-1, keepdims=True)
    byte = np.maximum(np.where(amax > 0, np.frexp(amax)[1] - 1 + 127, 0) - down, 1)
    scale = np.exp2(byte - 127.0)
    codes = (blocks / scale).astype(np.float32).astype(dtype).astype(np.float64)
    return np.moveaxis((codes * scale).reshape(v.shape), -1, axis)


WIDE = False


def mx_kscale(k):
    if not WIDE:
        return np.ones(k)
    levels = np.array([10, -10, 5, -5, 0])
    if k % 512:
        return np.exp2(np.random.permutation(np.resize(levels, k // 32))).repeat(32)
    a = np.empty((k // 512, 16))
    for p in range(k // 512):
        a[p, :8] = np.random.permutation(np.resize(levels, 8))
        for g in range(8):
            far = levels[np.abs(levels - a[p, g]) >= 10]
            a[p, g + 8] = far[np.random.randint(len(far))]
    return np.exp2(a.ravel()).repeat(32)


def f64(x):
    return np.asarray(x).astype(np.float64)


def striped8(idx):
    return np.asarray(idx).reshape(8, -1, 16).transpose(0, 2, 1).reshape(128, -1).astype(np.uint16)


def unstriped8(offs):
    return offs.reshape(8, 16, -1).transpose(0, 2, 1).reshape(8, -1).astype(np.int64)


def pick8(x, idx, run):
    r = np.arange(len(x))
    return x[r[:, None], idx[r % (8 * run) // run]]


E2M1 = np.array([0.0, 0.5, 1.0, 1.5, 2.0, 3.0, 4.0, 6.0, -0.0, -0.5, -1.0, -1.5, -2.0, -3.0, -4.0, -6.0])


def pack_weight(w, fmt):
    k, n = w.shape
    w = f64(np.asarray(w, np.float32).astype(ml_dtypes.bfloat16)).reshape(k // 32, 32, n)
    amax = np.abs(w).max(1)
    if fmt == "e4m3":
        byte = np.frexp(amax)[1] - 1 + 127 - 7
    else:
        mant, ex = np.frexp(amax / 6.0)
        byte = np.where(mant > 0.5, ex, ex - 1) + 127
    byte = np.clip(np.where(amax > 0, byte, 1), 1, 254)
    scaled = (w * np.exp2(127.0 - byte)[:, None, :]).reshape(k, n).astype(np.float32)
    by_word = np.ascontiguousarray(scaled.reshape(k // 512, 128, 4, n).transpose(0, 1, 3, 2))
    if fmt == "e4m3":
        words = by_word.astype(ml_dtypes.float8_e4m3fn).view(np.uint8)
    else:
        c = by_word.astype(ml_dtypes.float4_e2m1fn).view(np.uint8) & 0xF
        words = (c[..., 0::2] | (c[..., 1::2] << 4)).reshape(k // 512, 128, 2 * n)
    return np.ascontiguousarray(words), np.ascontiguousarray(byte.astype(np.uint8).reshape(k // 512, 16, n))


def unpack_weight(words, scales, fmt):
    g, _, n = scales.shape
    words = np.ascontiguousarray(words).reshape(g, 128, n, -1)
    if fmt == "e4m3":
        vals = words.view(ml_dtypes.float8_e4m3fn).astype(np.float64)
    else:
        nib = np.empty((g, 128, n, 4), np.uint8)
        nib[..., 0::2] = words & 0xF
        nib[..., 1::2] = words >> 4
        vals = E2M1[nib]
    vals = vals * np.repeat(np.exp2(scales.astype(np.float64) - 127.0), 8, axis=1)[..., None]
    return vals.transpose(0, 1, 3, 2).reshape(g * 512, n)


D, T, I, Q = 512, 1024, 512, 128


def setup_inputs():
    n = np.random.standard_normal
    idx = np.stack([np.random.permutation(T)[:I] for _ in range(8)])
    idx2 = np.stack([np.random.permutation(T)[:I] for _ in range(8)])
    idx3 = np.stack([np.random.permutation(T)[:I] for _ in range(8)])
    idx4 = np.stack([np.random.permutation(T)[:I] for _ in range(8)])
    fd = mx_kscale(D)
    keysp = pack_weight(n((D, T)) / fd[:, None], "e2m1")
    return {
        "query": (n((D, Q)) * 0.9 / np.sqrt(D) * fd[:, None]).astype(np.float32),
        "keys_words": keysp[0],
        "keys_scales": keysp[1],
        "lam": (np.random.uniform(0.3, 0.9, (Q, 1))).astype(np.float32),
        "old": (1.0 * n((Q, T))).astype(np.float32),
        "offs": striped8(idx),
        "offs2": striped8(idx2),
        "offs3": striped8(idx3),
        "offs4": striped8(idx4),
    }


def reference(query, keys_words, keys_scales, lam, old, offs, offs2, offs3, offs4):
    idx = unstriped8(offs)
    idx2 = unstriped8(offs2)
    idx3 = unstriped8(offs3)
    idx4 = unstriped8(offs4)
    keysu = unpack_weight(keys_words, keys_scales, "e2m1")
    queryq = mxq(f64(query), 0, "e4m3")
    a = queryq.T @ keysu
    w = pick8(a, idx, 16) + np.maximum(pick8(a, idx2, 16), pick8(a, idx3, 16)) * f64(lam)
    f1 = np.zeros((Q, T))
    f1[np.arange(Q)[:, None], idx[np.arange(Q) % 128 // 16]] = w
    f2 = f1 + f64(old)
    y = pick8(f2, idx4, 16)
    return y

@@ -1,0 +1,118 @@
+from contextlib import ExitStack
+
+import concourse.mybir as mybir
+
+F32 = mybir.dt.float32
+BF16 = mybir.dt.bfloat16
+I32 = mybir.dt.int32
+U32 = mybir.dt.uint32
+U16 = mybir.dt.uint16
+U8 = mybir.dt.uint8
+FP8X4 = mybir.dt.float8_e4m3fn_x4
+FP4X4 = mybir.dt.float4_e2m1fn_x4
+ALU = mybir.AluOpType
+COPY = mybir.ActivationFunctionType.Copy
+
+P = 128
+D, T, I, Q = 512, 1024, 512, 128
+PACK = 4
+N_PASS = 256
+HALF = I // 2
+
+FLOPS = 2 * D * T * Q
+
+
+def tile_attend_lookahead_lean_through_heads_kernel(
+    tc, query, keys_words, keys_scales, lam, old, offs, offs2, offs3, offs4, out
+):
+    nc = tc.nc
+    with ExitStack() as ctx:
+        keep = ctx.enter_context(tc.tile_pool(name="keep", bufs=1))
+        psum = ctx.enter_context(tc.psum_pool(name="psum", bufs=1))
+
+        token_list = keep.tile([P, I // 16], U16, name="token_list")
+        first_list = keep.tile([P, I // 16], U16, name="first_list")
+        second_list = keep.tile([P, I // 16], U16, name="second_list")
+        out_list = keep.tile([P, I // 16], U16, name="out_list")
+        q_raw = keep.tile([P, PACK, Q], F32, name="q_raw")
+        q_grouped = keep.tile([P, Q, PACK], BF16, name="q_grouped", align_bytes=64)
+        q_codes = keep.tile([P, Q], U32, name="q_codes", align_bytes=64)
+        q_scales = keep.tile([P, Q], U8, name="q_scales", align_bytes=64)
+        k_words = keep.tile([P, 2 * T], U8, name="k_words", align_bytes=64)
+        k_scales = keep.tile([P, T], U8, name="k_scales", align_bytes=64)
+        lam_col = keep.tile([P, 1], F32, name="lam_col")
+        old_rows = keep.tile([P, T], F32, name="old_rows")
+        scores = keep.tile([P, T], F32, name="scores")
+        placed = keep.tile([P, T], F32, name="placed")
+        totals = keep.tile([P, T], F32, name="totals")
+
+        nc.vector.memset(k_scales[:].bitcast(I32), 0)
+        nc.vector.memset(placed[:], 0.0)
+
+        nc.sync.dma_start(out=q_raw[:], in_=query.rearrange("(p j) q -> p j q", j=PACK))
+        for quad in range(4):
+            nc.scalar.dma_start(
+                out=k_scales[32 * quad : 32 * quad + 4, :].bitcast(I32),
+                in_=keys_scales[0, 4 * quad : 4 * quad + 4, :].bitcast(I32),
+            )
+        nc.sync.dma_start(out=k_words[:].bitcast(I32), in_=keys_words[0].bitcast(I32))
+        nc.sync.dma_start(first_list[:], offs2)
+        nc.sync.dma_start(second_list[:], offs3)
+        nc.sync.dma_start(token_list[:], offs)
+        nc.sync.dma_start(out=lam_col[:], in_=lam)
+        nc.sync.dma_start(out=old_rows[:], in_=old)
+        nc.sync.dma_start(out_list[:], offs4)
+
+        nc.vector.tensor_copy(out=q_grouped[:], in_=q_raw[:].rearrange("p j q -> p q j"))
+        nc.vector.quantize_mx(
+            out=q_codes[:].bitcast(FP8X4),
+            scales=q_scales[:],
+            in_=q_grouped[:].rearrange("p q j -> p (q j)"),
+        )
+
+        for n in range(T // N_PASS):
+            cols = slice(n * N_PASS, (n + 1) * N_PASS)
+            bank = psum.tile([P, N_PASS], F32, name="bank%d" % n)
+            nc.tensor.matmul_mx(
+                out=bank[:],
+                lhsT=q_codes[:].bitcast(FP8X4),
+                lhsT_scale=q_scales[:],
+                rhs=k_words[:, 2 * n * N_PASS : 2 * (n + 1) * N_PASS].bitcast(FP4X4),
+                rhs_scale=k_scales[:, cols],
+                start=True,
+                stop=True,
+            )
+            if n % 2 == 0:
+                nc.vector.tensor_copy(out=scores[:, cols], in_=bank[:])
+            else:
+                nc.scalar.copy(out=scores[:, cols], in_=bank[:])
+
+        halves = range(I // HALF)
+        entries = [slice(h * HALF // 16, (h + 1) * HALF // 16) for h in halves]
+        token = [keep.tile([P, HALF], F32, name="token%d" % h) for h in halves]
+        first = [keep.tile([P, HALF], F32, name="first%d" % h) for h in halves]
+        second = [keep.tile([P, HALF], F32, name="second%d" % h) for h in halves]
+        larger = [keep.tile([P, HALF], F32, name="larger%d" % h) for h in halves]
+        leaned = [keep.tile([P, HALF], F32, name="leaned%d" % h) for h in halves]
+        result = [keep.tile([P, HALF], F32, name="result%d" % h) for h in halves]
+
+        for h in halves:
+            nc.vector.tensor_copy(out=first[h][:], in_=scores[:].indirect(first_list[:, entries[h]]))
+            nc.scalar.activation(second[h][:], scores[:].indirect(second_list[:, entries[h]]), COPY)
+        for h in halves:
+            nc.scalar.activation(token[h][:], scores[:].indirect(token_list[:, entries[h]]), COPY)
+        for h in halves:
+            nc.vector.tensor_tensor(larger[h][:], first[h][:], second[h][:], ALU.max)
+        for h in halves:
+            nc.vector.tensor_scalar(leaned[h][:], larger[h][:], lam_col[:], None, ALU.mult)
+        for h in halves:
+            nc.vector.tensor_tensor(
+                placed[:].indirect(token_list[:, entries[h]]), token[h][:], leaned[h][:], ALU.add
+            )
+
+        nc.vector.tensor_tensor(totals[:], placed[:], old_rows[:], ALU.add)
+
+        nc.vector.tensor_copy(out=result[0][:], in_=totals[:].indirect(out_list[:, entries[0]]))
+        nc.scalar.activation(result[1][:], totals[:].indirect(out_list[:, entries[1]]), COPY)
+        nc.sync.dma_start(out=out[:, 0:HALF], in_=result[0][:])
+        nc.scalar.dma_start(out=out[:, HALF:I], in_=result[1][:])

@@ -16,7 +16,8 @@ COPY = mybir.ActivationFunctionType.Copy
 P = 128
 D, T, I, Q = 512, 1024, 512, 128
 PACK = 4
-N_PASS = 256
+PASS_WIDTHS = (256, 256, 256, 128, 128)
+Q_SPLIT = 88
 HALF = I // 2
 
 FLOPS = 2 * D * T * Q
@@ -50,12 +51,12 @@ def tile_attend_lookahead_lean_through_heads_kernel(
         nc.vector.memset(placed[:], 0.0)
 
         nc.sync.dma_start(out=q_raw[:], in_=query.rearrange("(p j) q -> p j q", j=PACK))
+        nc.sync.dma_start(out=k_words[:].bitcast(I32), in_=keys_words[0].bitcast(I32))
         for quad in range(4):
-            nc.scalar.dma_start(
+            nc.sync.dma_start(
                 out=k_scales[32 * quad : 32 * quad + 4, :].bitcast(I32),
                 in_=keys_scales[0, 4 * quad : 4 * quad + 4, :].bitcast(I32),
             )
-        nc.sync.dma_start(out=k_words[:].bitcast(I32), in_=keys_words[0].bitcast(I32))
         nc.sync.dma_start(first_list[:], offs2)
         nc.sync.dma_start(second_list[:], offs3)
         nc.sync.dma_start(token_list[:], offs)
@@ -63,21 +64,24 @@ def tile_attend_lookahead_lean_through_heads_kernel(
         nc.sync.dma_start(out=old_rows[:], in_=old)
         nc.sync.dma_start(out_list[:], offs4)
 
-        nc.vector.tensor_copy(out=q_grouped[:], in_=q_raw[:].rearrange("p j q -> p q j"))
+        q_view = q_raw[:].rearrange("p j q -> p q j")
+        nc.vector.tensor_copy(out=q_grouped[:, 0:Q_SPLIT, :], in_=q_view[:, 0:Q_SPLIT, :])
+        nc.scalar.copy(out=q_grouped[:, Q_SPLIT:Q, :], in_=q_view[:, Q_SPLIT:Q, :])
         nc.vector.quantize_mx(
             out=q_codes[:].bitcast(FP8X4),
             scales=q_scales[:],
             in_=q_grouped[:].rearrange("p q j -> p (q j)"),
         )
 
-        for n in range(T // N_PASS):
-            cols = slice(n * N_PASS, (n + 1) * N_PASS)
-            bank = psum.tile([P, N_PASS], F32, name="bank%d" % n)
+        for n, width in enumerate(PASS_WIDTHS):
+            begin = sum(PASS_WIDTHS[:n])
+            cols = slice(begin, begin + width)
+            bank = psum.tile([P, width], F32, name="bank%d" % n)
             nc.tensor.matmul_mx(
                 out=bank[:],
                 lhsT=q_codes[:].bitcast(FP8X4),
                 lhsT_scale=q_scales[:],
-                rhs=k_words[:, 2 * n * N_PASS : 2 * (n + 1) * N_PASS].bitcast(FP4X4),
+                rhs=k_words[:, 2 * begin : 2 * (begin + width)].bitcast(FP4X4),
                 rhs_scale=k_scales[:, cols],
                 start=True,
                 stop=True,
@@ -89,26 +93,22 @@ def tile_attend_lookahead_lean_through_heads_kernel(
 
         halves = range(I // HALF)
         entries = [slice(h * HALF // 16, (h + 1) * HALF // 16) for h in halves]
-        token = [keep.tile([P, HALF], F32, name="token%d" % h) for h in halves]
+        token = keep.tile([P, I], F32, name="token")
+        leaned = keep.tile([P, I], F32, name="leaned")
         first = [keep.tile([P, HALF], F32, name="first%d" % h) for h in halves]
         second = [keep.tile([P, HALF], F32, name="second%d" % h) for h in halves]
         larger = [keep.tile([P, HALF], F32, name="larger%d" % h) for h in halves]
-        leaned = [keep.tile([P, HALF], F32, name="leaned%d" % h) for h in halves]
         result = [keep.tile([P, HALF], F32, name="result%d" % h) for h in halves]
 
         for h in halves:
             nc.vector.tensor_copy(out=first[h][:], in_=scores[:].indirect(first_list[:, entries[h]]))
             nc.scalar.activation(second[h][:], scores[:].indirect(second_list[:, entries[h]]), COPY)
-        for h in halves:
-            nc.scalar.activation(token[h][:], scores[:].indirect(token_list[:, entries[h]]), COPY)
+        nc.scalar.activation(token[:], scores[:].indirect(token_list[:]), COPY)
         for h in halves:
             nc.vector.tensor_tensor(larger[h][:], first[h][:], second[h][:], ALU.max)
         for h in halves:
-            nc.vector.tensor_scalar(leaned[h][:], larger[h][:], lam_col[:], None, ALU.mult)
-        for h in halves:
-            nc.vector.tensor_tensor(
-                placed[:].indirect(token_list[:, entries[h]]), token[h][:], leaned[h][:], ALU.add
-            )
+            nc.vector.tensor_scalar(leaned[:, h * HALF : (h + 1) * HALF], larger[h][:], lam_col[:], None, ALU.mult)
+        nc.vector.tensor_tensor(placed[:].indirect(token_list[:]), token[:], leaned[:], ALU.add)
 
         nc.vector.tensor_tensor(totals[:], placed[:], old_rows[:], ALU.add)
 

from contextlib import ExitStack

import concourse.mybir as mybir

F32 = mybir.dt.float32
BF16 = mybir.dt.bfloat16
I32 = mybir.dt.int32
U32 = mybir.dt.uint32
U16 = mybir.dt.uint16
U8 = mybir.dt.uint8
FP8X4 = mybir.dt.float8_e4m3fn_x4
FP4X4 = mybir.dt.float4_e2m1fn_x4
ALU = mybir.AluOpType
COPY = mybir.ActivationFunctionType.Copy

P = 128
D, T, I, Q = 512, 1024, 512, 128
PACK = 4
PASS_WIDTHS = (256, 256, 256, 128, 128)
Q_SPLIT = 88
HALF = I // 2

FLOPS = 2 * D * T * Q


def tile_attend_lookahead_lean_through_heads_kernel(
    tc, query, keys_words, keys_scales, lam, old, offs, offs2, offs3, offs4, out
):
    nc = tc.nc
    with ExitStack() as ctx:
        keep = ctx.enter_context(tc.tile_pool(name="keep", bufs=1))
        psum = ctx.enter_context(tc.psum_pool(name="psum", bufs=1))

        token_list = keep.tile([P, I // 16], U16, name="token_list")
        first_list = keep.tile([P, I // 16], U16, name="first_list")
        second_list = keep.tile([P, I // 16], U16, name="second_list")
        out_list = keep.tile([P, I // 16], U16, name="out_list")
        q_raw = keep.tile([P, PACK, Q], F32, name="q_raw")
        q_grouped = keep.tile([P, Q, PACK], BF16, name="q_grouped", align_bytes=64)
        q_codes = keep.tile([P, Q], U32, name="q_codes", align_bytes=64)
        q_scales = keep.tile([P, Q], U8, name="q_scales", align_bytes=64)
        k_words = keep.tile([P, 2 * T], U8, name="k_words", align_bytes=64)
        k_scales = keep.tile([P, T], U8, name="k_scales", align_bytes=64)
        lam_col = keep.tile([P, 1], F32, name="lam_col")
        old_rows = keep.tile([P, T], F32, name="old_rows")
        scores = keep.tile([P, T], F32, name="scores")
        placed = keep.tile([P, T], F32, name="placed")
        totals = keep.tile([P, T], F32, name="totals")

        nc.vector.memset(k_scales[:].bitcast(I32), 0)
        nc.vector.memset(placed[:], 0.0)

        nc.sync.dma_start(out=q_raw[:], in_=query.rearrange("(p j) q -> p j q", j=PACK))
        nc.sync.dma_start(out=k_words[:].bitcast(I32), in_=keys_words[0].bitcast(I32))
        for quad in range(4):
            nc.sync.dma_start(
                out=k_scales[32 * quad : 32 * quad + 4, :].bitcast(I32),
                in_=keys_scales[0, 4 * quad : 4 * quad + 4, :].bitcast(I32),
            )
        nc.sync.dma_start(first_list[:], offs2)
        nc.sync.dma_start(second_list[:], offs3)
        nc.sync.dma_start(token_list[:], offs)
        nc.sync.dma_start(out=lam_col[:], in_=lam)
        nc.sync.dma_start(out=old_rows[:], in_=old)
        nc.sync.dma_start(out_list[:], offs4)

        q_view = q_raw[:].rearrange("p j q -> p q j")
        nc.vector.tensor_copy(out=q_grouped[:, 0:Q_SPLIT, :], in_=q_view[:, 0:Q_SPLIT, :])
        nc.scalar.copy(out=q_grouped[:, Q_SPLIT:Q, :], in_=q_view[:, Q_SPLIT:Q, :])
        nc.vector.quantize_mx(
            out=q_codes[:].bitcast(FP8X4),
            scales=q_scales[:],
            in_=q_grouped[:].rearrange("p q j -> p (q j)"),
        )

        for n, width in enumerate(PASS_WIDTHS):
            begin = sum(PASS_WIDTHS[:n])
            cols = slice(begin, begin + width)
            bank = psum.tile([P, width], F32, name="bank%d" % n)
            nc.tensor.matmul_mx(
                out=bank[:],
                lhsT=q_codes[:].bitcast(FP8X4),
                lhsT_scale=q_scales[:],
                rhs=k_words[:, 2 * begin : 2 * (begin + width)].bitcast(FP4X4),
                rhs_scale=k_scales[:, cols],
                start=True,
                stop=True,
            )
            if n % 2 == 0:
                nc.vector.tensor_copy(out=scores[:, cols], in_=bank[:])
            else:
                nc.scalar.copy(out=scores[:, cols], in_=bank[:])

        halves = range(I // HALF)
        entries = [slice(h * HALF // 16, (h + 1) * HALF // 16) for h in halves]
        token = keep.tile([P, I], F32, name="token")
        leaned = keep.tile([P, I], F32, name="leaned")
        first = [keep.tile([P, HALF], F32, name="first%d" % h) for h in halves]
        second = [keep.tile([P, HALF], F32, name="second%d" % h) for h in halves]
        larger = [keep.tile([P, HALF], F32, name="larger%d" % h) for h in halves]
        result = [keep.tile([P, HALF], F32, name="result%d" % h) for h in halves]

        for h in halves:
            nc.vector.tensor_copy(out=first[h][:], in_=scores[:].indirect(first_list[:, entries[h]]))
            nc.scalar.activation(second[h][:], scores[:].indirect(second_list[:, entries[h]]), COPY)
        nc.scalar.activation(token[:], scores[:].indirect(token_list[:]), COPY)
        for h in halves:
            nc.vector.tensor_tensor(larger[h][:], first[h][:], second[h][:], ALU.max)
        for h in halves:
            nc.vector.tensor_scalar(leaned[:, h * HALF : (h + 1) * HALF], larger[h][:], lam_col[:], None, ALU.mult)
        nc.vector.tensor_tensor(placed[:].indirect(token_list[:]), token[:], leaned[:], ALU.add)

        nc.vector.tensor_tensor(totals[:], placed[:], old_rows[:], ALU.add)

        nc.vector.tensor_copy(out=result[0][:], in_=totals[:].indirect(out_list[:, entries[0]]))
        nc.scalar.activation(result[1][:], totals[:].indirect(out_list[:, entries[1]]), COPY)
        nc.sync.dma_start(out=out[:, 0:HALF], in_=result[0][:])
        nc.scalar.dma_start(out=out[:, HALF:I], in_=result[1][:])
